import numpy as np
import ml_dtypes


def mxq(x, axis, fmt="e4m3"):
    dtype, down = {"e4m3": (ml_dtypes.float8_e4m3fn, 7), "e5m2": (ml_dtypes.float8_e5m2, 14)}[fmt]
    v = np.moveaxis(np.asarray(x, np.float32).astype(ml_dtypes.bfloat16).astype(np.float64), axis, -1)
    blocks = v.reshape(v.shape[:-1] + (-1, 32))
    amax = np.abs(blocks).max(-1, keepdims=True)
    byte = np.maximum(np.where(amax > 0, np.frexp(amax)[1] - 1 + 127, 0) - down, 1)
    scale = np.exp2(byte - 127.0)
    codes = (blocks / scale).astype(np.float32).astype(dtype).astype(np.float64)
    return np.moveaxis((codes * scale).reshape(v.shape), -1, axis)


WIDE = False


def mx_kscale(k):
    if not WIDE:
        return np.ones(k)
    levels = np.array([10, -10, 5, -5, 0])
    if k % 512:
        return np.exp2(np.random.permutation(np.resize(levels, k // 32))).repeat(32)
    a = np.empty((k // 512, 16))
    for p in range(k // 512):
        a[p, :8] = np.random.permutation(np.resize(levels, 8))
        for g in range(8):
            far = levels[np.abs(levels - a[p, g]) >= 10]
            a[p, g + 8] = far[np.random.randint(len(far))]
    return np.exp2(a.ravel()).repeat(32)


BF16 = ml_dtypes.bfloat16


def bf(x):
    return np.asarray(x, np.float32).astype(BF16)


def f64(x):
    return np.asarray(x).astype(np.float64)


E2M1 = np.array([0.0, 0.5, 1.0, 1.5, 2.0, 3.0, 4.0, 6.0, -0.0, -0.5, -1.0, -1.5, -2.0, -3.0, -4.0, -6.0])


def pack_weight(w, fmt):
    k, n = w.shape
    w = f64(bf(w)).reshape(k // 32, 32, n)
    amax = np.abs(w).max(1)
    if fmt == "e4m3":
        byte = np.frexp(amax)[1] - 1 + 127 - 7
    else:
        mant, ex = np.frexp(amax / 6.0)
        byte = np.where(mant > 0.5, ex, ex - 1) + 127
    byte = np.clip(np.where(amax > 0, byte, 1), 1, 254)
    scaled = (w * np.exp2(127.0 - byte)[:, None, :]).reshape(k, n).astype(np.float32)
    by_word = np.ascontiguousarray(scaled.reshape(k // 512, 128, 4, n).transpose(0, 1, 3, 2))
    if fmt == "e4m3":
        words = by_word.astype(ml_dtypes.float8_e4m3fn).view(np.uint8)
    else:
        c = by_word.astype(ml_dtypes.float4_e2m1fn).view(np.uint8) & 0xF
        words = c[..., 0::2] | (c[..., 1::2] << 4)
    return np.ascontiguousarray(words), np.ascontiguousarray(byte.astype(np.uint8).reshape(k // 512, 16, n))


def unpack_weight(words, scales, fmt):
    g, p, n, _ = words.shape
    if fmt == "e4m3":
        vals = np.ascontiguousarray(words).view(ml_dtypes.float8_e4m3fn).astype(np.float64)
    else:
        nib = np.empty((g, p, n, 4), np.uint8)
        nib[..., 0::2] = words & 0xF
        nib[..., 1::2] = words >> 4
        vals = E2M1[nib]
    vals = vals * np.repeat(np.exp2(scales.astype(np.float64) - 127.0), 8, axis=1)[..., None]
    return vals.transpose(0, 1, 3, 2).reshape(g * 512, n)
def pack4(w):
    words, scales = pack_weight(w, "e2m1")
    return words.reshape(words.shape[0], 128, -1), scales


def unpack4(words, scales):
    return unpack_weight(words.reshape(words.shape[0], 128, -1, 2), scales, "e2m1")


NO, NV, X, P, Q, S = 512, 1024, 1024, 1024, 1536, 512
CORE = 0.15


def setup_inputs():
    so, sv, sx = mx_kscale(NO), mx_kscale(NV), mx_kscale(X)
    t = mx_kscale(Q)
    l_words, l_scales = pack4(CORE * np.random.standard_normal((X, Q)) / np.sqrt(X) * sx[:, None] / t)
    r_words, r_scales = pack4(np.random.standard_normal((X, S)) / sx[:, None])
    return {"xo_bra": bf(np.random.standard_normal((NO, P)) / np.sqrt(NO) / so[:, None]),
            "xo_ket": bf(np.random.standard_normal((NO, Q)) * so[:, None]),
            "d_occ": bf(2.0 * np.exp(-1.5 * np.random.random(NO))),
            "xv_bra": bf(np.random.standard_normal((NV, P)) / np.sqrt(NV) / sv[:, None]),
            "xv_ket": bf(np.random.standard_normal((NV, Q)) * sv[:, None] * t),
            "d_vir": bf(np.exp(-2.0 * np.random.random(NV))),
            "l_words": l_words, "l_scales": l_scales,
            "r_words": r_words, "r_scales": r_scales}


def reference(xo_bra, xo_ket, d_occ, xv_bra, xv_ket, d_vir, l_words, l_scales, r_words, r_scales):
    bo = f64(xo_bra) * f64(d_occ)[:, None]
    bv = f64(xv_bra) * f64(d_vir)[:, None]
    occ = mxq(bo, 0, "e4m3").T @ mxq(f64(xo_ket), 0, "e4m3")
    vir = mxq(bv, 0, "e4m3").T @ mxq(f64(xv_ket), 0, "e4m3")
    a = occ * vir
    z = unpack4(l_words, l_scales).T @ unpack4(r_words, r_scales)
    return mxq(a, 1, "e4m3") @ mxq(z, 0, "e4m3")

@@ -1,0 +1,317 @@
+from contextlib import ExitStack
+
+import concourse.mybir as mybir
+
+NO, NV, X, NB, NK, S = 512, 1024, 1024, 1024, 1536, 512
+FLOPS = 2 * (NO + NV) * NB * NK + 2 * X * NK * S + 2 * NB * NK * S
+
+F32 = mybir.dt.float32
+BF16 = mybir.dt.bfloat16
+I32 = mybir.dt.int32
+U32 = mybir.dt.uint32
+U8 = mybir.dt.uint8
+FP8X4 = mybir.dt.float8_e4m3fn_x4
+FP4X4 = mybir.dt.float4_e2m1fn_x4
+MULT = mybir.AluOpType.mult
+
+P = 128
+PACK = 4
+KP = P * PACK
+GROUPS = NK // KP
+PASSES = (NO + NV) // KP
+XP = X // KP
+HALVES = NB // KP
+TILES = NB // P
+RUN = 4
+
+LOADS = "k10 k20 d b10 b20 s0 k00 s1 b00 s2 R s3 L0 k11 L1 k21 L2 k01 k12 k22 b11 b21 k02 b01"
+HEAD = 6
+PERIOD = 4
+LAG = 10
+ZPOS = 2
+ZSTEP = 12
+OLAG = 5
+VIR_BUFS = 7
+ALLV = "k11 k21 k12 k22"
+ALLS = "k02 b01"
+PERM_AT = 4
+RAW_BUFS = 15
+ZQ_AT = 28
+
+
+def tile_thc_laplace_mp2_s12_kernel(
+    tc, xo_bra, xo_ket, d_occ, xv_bra, xv_ket, d_vir, l_words, l_scales, r_words, r_scales, out
+):
+    nc = tc.nc
+    ket_rows = [xo_ket, xv_ket[0:KP, :], xv_ket[KP:, :]]
+    bra_rows = [xo_bra, xv_bra[0:KP, :], xv_bra[KP:, :]]
+
+    with ExitStack() as ctx:
+        keep = ctx.enter_context(tc.tile_pool(name="keep", bufs=1))
+        work = ctx.enter_context(tc.tile_pool(name="work", bufs=3))
+        psum = ctx.enter_context(tc.psum_pool(name="psum", bufs=1))
+        ctx.enter_context(tc.manual_schedule())
+
+        l_raw = {}
+        l_rows = keep.tile([P, XP, NK], U8, name="l_rows", align_bytes=64)
+        r_codes = keep.tile([P, XP, 2 * S], U8, name="r_codes", align_bytes=64)
+        r_plane = keep.tile([P, XP, S], U8, name="r_plane", align_bytes=64)
+        d_o = keep.tile([P, PACK], BF16, name="d_o")
+        d_v = keep.tile([P, XP, PACK], BF16, name="d_v")
+        damping = [d_o[:, :], d_v[:, 0, :], d_v[:, 1, :]]
+
+        nc.vector.memset(l_rows[:].rearrange("p g n -> p (g n)").bitcast(I32), 0)
+        nc.vector.memset(r_plane[:].rearrange("p g n -> p (g n)").bitcast(I32), 0)
+
+        raw = {}
+
+        def load(key):
+            if key[0] == "s":
+                r = int(key[1])
+                nc.sync.dma_start(
+                    out=l_rows[r:P:32, :, :].bitcast(I32),
+                    in_=l_scales[:, r:16:4, :].rearrange("g q n -> q g n").bitcast(I32),
+                )
+                nc.sync.dma_start(
+                    out=r_plane[r:P:32, :, :].bitcast(I32),
+                    in_=r_scales[:, r:16:4, :].rearrange("g q n -> q g n").bitcast(I32),
+                )
+            elif key[0] == "L":
+                g = int(key[1])
+                l_raw[g] = keep.tile([P, XP, 2 * KP], U8, name="l_raw%d" % g, align_bytes=64)
+                nc.sync.dma_start(
+                    out=l_raw[g][:].bitcast(I32),
+                    in_=l_words[:, :, 2 * KP * g : 2 * KP * (g + 1)].rearrange("g p n -> p g n").bitcast(I32),
+                )
+            elif key == "R":
+                nc.sync.dma_start(out=r_codes[:].bitcast(I32), in_=r_words.rearrange("g p n -> p g n").bitcast(I32))
+            elif key == "d":
+                nc.sync.dma_start(out=d_o[:], in_=d_occ.rearrange("(p j) -> p j", j=PACK))
+                nc.sync.dma_start(out=d_v[:], in_=d_vir.rearrange("(g p j) -> p g j", p=P, j=PACK))
+            else:
+                rows = (ket_rows if key[0] == "k" else bra_rows)[int(key[1])]
+                c0 = KP * int(key[2])
+                raw[key] = work.tile([P, PACK, KP], BF16, name="raw_" + key, tag="raw", bufs=RAW_BUFS, align_bytes=64)
+                nc.sync.dma_start(out=raw[key][:], in_=rows[:, c0 : c0 + KP].rearrange("(p j) w -> p j w", j=PACK))
+
+        to_load = LOADS.split()
+
+        def load_ahead(done):
+            while to_load and (to_load[0][0] not in "kb" or len(raw) < done + RAW_BUFS):
+                load(to_load.pop(0))
+
+        load_ahead(0)
+
+        grouped = {}
+        codes = {}
+        planes = {}
+        l_codes = {}
+        l_plane = {}
+        z_bf = {}
+
+        def damp(key):
+            damped = work.tile([P, PACK, KP], BF16, name="damped", align_bytes=64)
+            for j in range(PACK):
+                nc.vector.tensor_scalar(
+                    out=damped[:, j, :], in0=raw[key][:, j, :], scalar1=damping[int(key[1])][:, j : j + 1],
+                    scalar2=None, op0=MULT,
+                )
+            raw[key] = damped
+
+        def interleave(key, half):
+            piece = key + str(half)
+            grouped[piece] = work.tile([P, 2 * KP], BF16, name="grouped", bufs=6, align_bytes=64)
+            if key[0] == "k":
+                src = raw[key][:].rearrange("p j (m t i) -> p m t j i", t=PACK, i=RUN)[:, :, 2 * half : 2 * half + 2, :, :]
+                dst = grouped[piece][:].rearrange("p (t m i j) -> p m t j i", t=2, i=RUN, j=PACK)
+            else:
+                src = raw[key][:, :, 2 * P * half : 2 * P * (half + 1)].rearrange("p j (c i) -> p c j i", i=RUN)
+                dst = grouped[piece][:].rearrange("p (c i j) -> p c j i", i=RUN, j=PACK)
+            if (half == 1 and key not in ALLV.split()) or key in ALLS.split():
+                nc.scalar.copy(out=dst, in_=src)
+            else:
+                nc.vector.tensor_copy(out=dst, in_=src)
+
+        def quantize(key, values, width):
+            codes[key] = keep.tile([P, width], U32, name="codes_" + key, align_bytes=64)
+            planes[key] = keep.tile([P, width], U8, name="plane_" + key, align_bytes=64)
+            nc.vector.quantize_mx(out=codes[key][:].bitcast(FP8X4), scales=planes[key][:], in_=values)
+
+        def permute_l(g):
+            l_codes[g] = keep.tile([P, XP, PACK, 2 * P], U8, name="l_codes%d" % g, align_bytes=64)
+            l_plane[g] = keep.tile([P, XP, PACK, P], U8, name="l_plane%d" % g, align_bytes=64)
+            nc.vector.tensor_copy(
+                out=l_codes[g][:].bitcast(I32).rearrange("p x t (m w) -> p x t m w", w=2),
+                in_=l_raw[g][:].bitcast(I32).rearrange("p x (m t w) -> p x t m w", t=PACK, w=2),
+            )
+            nc.vector.tensor_copy(
+                out=l_plane[g][:].bitcast(I32),
+                in_=l_rows[:, :, KP * g : KP * (g + 1)].bitcast(I32).rearrange("p x (m t) -> p x t m", t=PACK),
+            )
+
+        banks = {}
+        zq = []
+        vir_sb = {}
+        a_bf = {}
+
+        def bank(name):
+            return psum.tile([P, PACK, P], F32, name=name, tag="bank", bufs=8)
+
+        def pe(job):
+            kind = job[0]
+            if kind == "Z":
+                g, sc = int(job[1]), int(job[2])
+                banks[job] = bank("z_ps")
+                for t in range(PACK):
+                    for x in range(XP):
+                        nc.tensor.matmul_mx(
+                            out=banks[job][:, t, :],
+                            lhsT=l_codes[g][:, x, t, :].bitcast(FP4X4), lhsT_scale=l_plane[g][:, x, t, :],
+                            rhs=r_codes[:, x, 2 * P * sc : 2 * P * (sc + 1)].bitcast(FP4X4),
+                            rhs_scale=r_plane[:, x, P * sc : P * (sc + 1)],
+                            start=(x == 0), stop=(x == XP - 1),
+                        )
+            elif kind == "V":
+                g, q, tp = int(job[1]), int(job[2]), int(job[3])
+                banks[job] = psum.tile([P, 2, 2 * P], F32, name="vir_ps", tag="bank", bufs=8)
+                for t in range(2):
+                    for c in (1, 2):
+                        ket, bra = "k%d%d%d" % (c, g, tp), "b%d%d%d" % (c, q // 2, q % 2)
+                        nc.tensor.matmul_mx(
+                            out=banks[job][:, t, :],
+                            lhsT=codes[ket][:, P * t : P * (t + 1)].bitcast(FP8X4),
+                            lhsT_scale=planes[ket][:, P * t : P * (t + 1)],
+                            rhs=codes[bra][:].bitcast(FP8X4), rhs_scale=planes[bra][:],
+                            start=(c == 1), stop=(c == 2),
+                        )
+            elif kind == "C":
+                g, u = int(job[1]), int(job[2])
+                banks[job] = bank("occ_ps")
+                bra, cols = "b0%d%d" % (u // 4, u % 4 // 2), slice(P * (u % 2), P * (u % 2 + 1))
+                for t in range(PACK):
+                    ket, kc = "k0%d%d" % (g, t // 2), slice(P * (t % 2), P * (t % 2 + 1))
+                    nc.tensor.matmul_mx(
+                        out=banks[job][:, t, :],
+                        lhsT=codes[ket][:, kc].bitcast(FP8X4), lhsT_scale=planes[ket][:, kc],
+                        rhs=codes[bra][:, cols].bitcast(FP8X4), rhs_scale=planes[bra][:, cols],
+                        start=True, stop=True,
+                    )
+            else:
+                u = int(job[1])
+                banks[job] = bank("out_ps")
+                for g in range(GROUPS):
+                    a, z = "a%d%d" % (g, u), "z%d" % g
+                    nc.tensor.matmul_mx(
+                        out=banks[job][:].rearrange("p t n -> p (t n)"),
+                        lhsT=codes[a][:].bitcast(FP8X4), lhsT_scale=planes[a][:],
+                        rhs=codes[z][:].bitcast(FP8X4), rhs_scale=planes[z][:],
+                        start=(g == 0), stop=(g == GROUPS - 1),
+                    )
+
+        def drain(job):
+            kind = job[0]
+            if kind == "Z":
+                g, sc = int(job[1]), int(job[2])
+                if sc == 0:
+                    z_bf[g] = work.tile([P, S, PACK], BF16, name="z_bf", bufs=3, align_bytes=64)
+                nc.scalar.copy(out=z_bf[g][:, P * sc : P * (sc + 1), :], in_=banks[job][:].rearrange("p t n -> p n t"))
+            elif kind == "V":
+                if job[3] == "0":
+                    vir_sb[job[1:3]] = work.tile([P, 2, 2 * P, 2], F32, name="vir_sb", bufs=VIR_BUFS, align_bytes=64)
+                nc.scalar.copy(out=vir_sb[job[1:3]][:, int(job[3]), :, :], in_=banks[job][:].rearrange("p t n -> p n t"))
+            else:
+                u = int(job[1])
+                result = work.tile([P, PACK, P], F32, name="result", align_bytes=64)
+                nc.scalar.copy(out=result[:], in_=banks[job][:])
+                nc.sync.dma_start(out=out[P * u : P * (u + 1), :], in_=result[:].rearrange("p t n -> p (t n)"))
+
+        def product(job):
+            u = int(job[2])
+            a_bf[job] = work.tile([P, P, 2, 2], BF16, name="a_bf", bufs=4, align_bytes=64)
+            vir = vir_sb[job[1] + str(u // 2)][:, :, P * (u % 2) : P * (u % 2 + 1), :]
+            nc.vector.tensor_tensor(
+                out=a_bf[job][:],
+                in0=banks[job][:].rearrange("p (a b) n -> p n a b", b=2),
+                in1=vir.rearrange("p a n b -> p n a b"),
+                op=MULT,
+            )
+
+        def quant_a(job):
+            quantize("a" + job[1:], a_bf[job][:].rearrange("p n a b -> p (n a b)"), P)
+
+        chunks = [key for key in LOADS.split() if key[0] in "kb"]
+
+        def prep(k):
+            if k + 1 < len(chunks) and chunks[k + 1][0] == "b":
+                pre = chunks[k + 1]
+            else:
+                pre = None
+            if k < len(chunks):
+                interleave(chunks[k], 1)
+                interleave(chunks[k], 0)
+            if k > 0:
+                quantize(chunks[k - 1] + "1", grouped[chunks[k - 1] + "1"][:], 2 * P)
+            if pre:
+                damp(pre)
+            if k < len(chunks):
+                late.append(chunks[k] + "0")
+            load_ahead(k + 1)
+
+        late = []
+
+        def flush():
+            while late:
+                piece = late.pop(0)
+                quantize(piece, grouped[piece][:], 2 * P)
+
+        vir_jobs = ["V%d%d%d" % (g, q, tp) for g in range(GROUPS) for q in (0, 1) for tp in (0, 1)]
+        vir_jobs += ["V%d%d%d" % (g, q, tp) for q in (2, 3) for g in range(GROUPS) for tp in (0, 1)]
+        occ_jobs = ["C%d%d" % (g, u) for g in range(GROUPS) for u in range(4)]
+        occ_jobs += ["C%d%d" % (g, u) for u in range(4, TILES) for g in range(GROUPS)]
+        z_jobs = ["Z%d%d" % (g, sc) for g in range(GROUPS) for sc in range(PACK)]
+        jobs = []
+        outs = []
+        for i in range(len(vir_jobs) + LAG + OLAG + 1):
+            if i < len(vir_jobs):
+                jobs.append(vir_jobs[i])
+            if i >= ZPOS:
+                jobs.extend(z_jobs[ZSTEP * (i - ZPOS) : ZSTEP * (i - ZPOS + 1)])
+            if 0 <= i - LAG < len(occ_jobs):
+                jobs.append(occ_jobs[i - LAG])
+                if occ_jobs[i - LAG][1] == str(GROUPS - 1):
+                    outs.append((i + OLAG, "O" + occ_jobs[i - LAG][2]))
+            if outs and outs[0][0] <= i:
+                jobs.append(outs.pop(0)[1])
+
+        if chunks[0][0] == "b":
+            damp(chunks[0])
+        for k in range(HEAD):
+            prep(k)
+            flush()
+            if 0 <= k - PERM_AT < GROUPS:
+                permute_l(k - PERM_AT)
+        k = HEAD
+        pending = []
+        for n, job in enumerate(jobs):
+            if n % PERIOD == 0 and k <= len(chunks):
+                prep(k)
+                if 0 <= k - PERM_AT < GROUPS:
+                    permute_l(k - PERM_AT)
+                k = k + 1
+            if job[0] == "O":
+                while any(j[2] == job[1] for j in pending):
+                    quant_a(pending.pop(0))
+            pe(job)
+            if job[0] == "C":
+                product(job)
+                if pending:
+                    quant_a(pending.pop(0))
+                pending.append(job)
+            else:
+                drain(job)
+            flush()
+            if job[0] == "Z" and job[2] == "3":
+                zq.append(job[1])
+            elif zq and n >= ZQ_AT:
+                g = zq.pop(0)
+                quantize("z" + g, z_bf[int(g)][:].rearrange("p n t -> p (n t)"), S)

@@ -2,8 +2,8 @@ from contextlib import ExitStack
 
 import concourse.mybir as mybir
 
-NO, NV, X, NB, NK, S = 512, 1024, 1024, 1024, 1536, 512
-FLOPS = 2 * (NO + NV) * NB * NK + 2 * X * NK * S + 2 * NB * NK * S
+NO, NV, NX, NB, NK, NS = 512, 1024, 1024, 1024, 1536, 512
+FLOPS = 2 * (NO + NV) * NB * NK + 2 * NX * NK * NS + 2 * NB * NK * NS
 
 F32 = mybir.dt.float32
 BF16 = mybir.dt.bfloat16
@@ -15,303 +15,335 @@ FP4X4 = mybir.dt.float4_e2m1fn_x4
 MULT = mybir.AluOpType.mult
 
 P = 128
-PACK = 4
-KP = P * PACK
+SLOTS = 4
+KP = P * SLOTS
 GROUPS = NK // KP
-PASSES = (NO + NV) // KP
-XP = X // KP
-HALVES = NB // KP
+X_PASSES = NX // KP
 TILES = NB // P
 RUN = 4
+BANKS = 8
+OCC, VIR_A, VIR_B = 0, 1, 2
 
-LOADS = "k10 k20 d b10 b20 s0 k00 s1 b00 s2 R s3 L0 k11 L1 k21 L2 k01 k12 k22 b11 b21 k02 b01"
-HEAD = 6
-PERIOD = 4
-LAG = 10
-ZPOS = 2
-ZSTEP = 12
-OLAG = 5
-VIR_BUFS = 7
-ALLV = "k11 k21 k12 k22"
-ALLS = "k02 b01"
-PERM_AT = 4
-RAW_BUFS = 15
-ZQ_AT = 28
+SCALAR_HEAD = 5
+FIRST_BANKS = 4
+LATE_START = 14
+LATE_EVERY = 5
+OCC_START = 21
+OUT_LAG = 5
+QUANT_LAG = 1
+DAMP_FIRST = 5
+OUT_START = 38
+PERM_AT = 6
+GROUPED_BUFS = 5
+VIR_BUFS = 9
 
 
 def tile_thc_laplace_mp2_s12_kernel(
     tc, xo_bra, xo_ket, d_occ, xv_bra, xv_ket, d_vir, l_words, l_scales, r_words, r_scales, out
 ):
     nc = tc.nc
-    ket_rows = [xo_ket, xv_ket[0:KP, :], xv_ket[KP:, :]]
-    bra_rows = [xo_bra, xv_bra[0:KP, :], xv_bra[KP:, :]]
+    rows_of = {
+        "ket": [xo_ket, xv_ket[0:KP, :], xv_ket[KP:, :]],
+        "bra": [xo_bra, xv_bra[0:KP, :], xv_bra[KP:, :]],
+    }
+    chunks = [
+        ("bra", VIR_A, 0), ("bra", VIR_B, 0), ("ket", VIR_A, 0), ("ket", VIR_B, 0),
+        ("bra", OCC, 0), ("ket", OCC, 0),
+        ("ket", VIR_A, 1), ("ket", VIR_B, 1), ("ket", VIR_A, 2), ("ket", VIR_B, 2),
+        ("bra", VIR_A, 1), ("bra", VIR_B, 1), ("ket", OCC, 1), ("ket", OCC, 2), ("bra", OCC, 1),
+    ]
+    scalar_early = chunks[0 : 2 * SCALAR_HEAD : 2]
+    scalar_late = chunks[-2:]
 
     with ExitStack() as ctx:
         keep = ctx.enter_context(tc.tile_pool(name="keep", bufs=1))
         work = ctx.enter_context(tc.tile_pool(name="work", bufs=3))
-        psum = ctx.enter_context(tc.psum_pool(name="psum", bufs=1))
+        psum = ctx.enter_context(tc.psum_pool(name="psum", bufs=BANKS))
         ctx.enter_context(tc.manual_schedule())
 
-        l_raw = {}
-        l_rows = keep.tile([P, XP, NK], U8, name="l_rows", align_bytes=64)
-        r_codes = keep.tile([P, XP, 2 * S], U8, name="r_codes", align_bytes=64)
-        r_plane = keep.tile([P, XP, S], U8, name="r_plane", align_bytes=64)
-        d_o = keep.tile([P, PACK], BF16, name="d_o")
-        d_v = keep.tile([P, XP, PACK], BF16, name="d_v")
+        l_rows = keep.tile([P, X_PASSES, NK], U8, name="l_rows", align_bytes=64)
+        r_plane = keep.tile([P, X_PASSES, NS], U8, name="r_plane", align_bytes=64)
+        nc.vector.memset(l_rows[:].rearrange("p x n -> p (x n)").bitcast(I32), 0)
+        nc.vector.memset(r_plane[:].rearrange("p x n -> p (x n)").bitcast(I32), 0)
+
+        r_codes = keep.tile([P, X_PASSES, 2 * NS], U8, name="r_codes", align_bytes=64)
+        d_o = keep.tile([P, SLOTS], BF16, name="d_o")
+        d_v = keep.tile([P, X_PASSES, SLOTS], BF16, name="d_v")
         damping = [d_o[:, :], d_v[:, 0, :], d_v[:, 1, :]]
-
-        nc.vector.memset(l_rows[:].rearrange("p g n -> p (g n)").bitcast(I32), 0)
-        nc.vector.memset(r_plane[:].rearrange("p g n -> p (g n)").bitcast(I32), 0)
-
         raw = {}
+        l_raw = {}
 
-        def load(key):
-            if key[0] == "s":
-                r = int(key[1])
+        def load_chunk(chunk):
+            side, c, part = chunk
+            raw[chunk] = keep.tile([P, SLOTS, KP], BF16, name="raw_%s%d%d" % chunk, align_bytes=64)
+            rows = rows_of[side][c][:, KP * part : KP * (part + 1)]
+            nc.sync.dma_start(out=raw[chunk][:], in_=rows.rearrange("(p j) w -> p j w", j=SLOTS))
+
+        def load_scale_rows(r):
+            for plane, scales in ((l_rows, l_scales), (r_plane, r_scales)):
                 nc.sync.dma_start(
-                    out=l_rows[r:P:32, :, :].bitcast(I32),
-                    in_=l_scales[:, r:16:4, :].rearrange("g q n -> q g n").bitcast(I32),
+                    out=plane[r:P:32, :, :].bitcast(I32),
+                    in_=scales[:, r:16:4, :].rearrange("x q n -> q x n").bitcast(I32),
                 )
-                nc.sync.dma_start(
-                    out=r_plane[r:P:32, :, :].bitcast(I32),
-                    in_=r_scales[:, r:16:4, :].rearrange("g q n -> q g n").bitcast(I32),
-                )
-            elif key[0] == "L":
-                g = int(key[1])
-                l_raw[g] = keep.tile([P, XP, 2 * KP], U8, name="l_raw%d" % g, align_bytes=64)
-                nc.sync.dma_start(
-                    out=l_raw[g][:].bitcast(I32),
-                    in_=l_words[:, :, 2 * KP * g : 2 * KP * (g + 1)].rearrange("g p n -> p g n").bitcast(I32),
-                )
-            elif key == "R":
-                nc.sync.dma_start(out=r_codes[:].bitcast(I32), in_=r_words.rearrange("g p n -> p g n").bitcast(I32))
-            elif key == "d":
-                nc.sync.dma_start(out=d_o[:], in_=d_occ.rearrange("(p j) -> p j", j=PACK))
-                nc.sync.dma_start(out=d_v[:], in_=d_vir.rearrange("(g p j) -> p g j", p=P, j=PACK))
-            else:
-                rows = (ket_rows if key[0] == "k" else bra_rows)[int(key[1])]
-                c0 = KP * int(key[2])
-                raw[key] = work.tile([P, PACK, KP], BF16, name="raw_" + key, tag="raw", bufs=RAW_BUFS, align_bytes=64)
-                nc.sync.dma_start(out=raw[key][:], in_=rows[:, c0 : c0 + KP].rearrange("(p j) w -> p j w", j=PACK))
 
-        to_load = LOADS.split()
+        def load_l(g):
+            l_raw[g] = keep.tile([P, X_PASSES, 2 * KP], U8, name="l_raw%d" % g, align_bytes=64)
+            words = l_words[:, :, 2 * KP * g : 2 * KP * (g + 1)]
+            nc.sync.dma_start(out=l_raw[g][:].bitcast(I32), in_=words.rearrange("x p n -> p x n").bitcast(I32))
 
-        def load_ahead(done):
-            while to_load and (to_load[0][0] not in "kb" or len(raw) < done + RAW_BUFS):
-                load(to_load.pop(0))
+        for k, chunk in enumerate(chunks):
+            load_chunk(chunk)
+            if k == 0:
+                nc.sync.dma_start(out=d_o[:], in_=d_occ.rearrange("(p j) -> p j", j=SLOTS))
+                nc.sync.dma_start(out=d_v[:], in_=d_vir.rearrange("(x p j) -> p x j", p=P, j=SLOTS))
+            if 0 <= k - (PERM_AT - 3) < 4:
+                load_scale_rows(k - (PERM_AT - 3))
+            if k == PERM_AT:
+                nc.sync.dma_start(out=r_codes[:].bitcast(I32), in_=r_words.rearrange("x p n -> p x n").bitcast(I32))
+            if k - PERM_AT in (0, 2, 4):
+                load_l((k - PERM_AT) // 2)
 
-        load_ahead(0)
+        grouped, codes, planes = {}, {}, {}
+        l_codes, l_plane, z_bf, vir_sb, a_bf, banks = {}, {}, {}, {}, {}, {}
 
-        grouped = {}
-        codes = {}
-        planes = {}
-        l_codes = {}
-        l_plane = {}
-        z_bf = {}
-
-        def damp(key):
-            damped = work.tile([P, PACK, KP], BF16, name="damped", align_bytes=64)
-            for j in range(PACK):
+        def damp(chunk):
+            for j in range(SLOTS):
                 nc.vector.tensor_scalar(
-                    out=damped[:, j, :], in0=raw[key][:, j, :], scalar1=damping[int(key[1])][:, j : j + 1],
-                    scalar2=None, op0=MULT,
+                    out=raw[chunk][:, j, :], in0=raw[chunk][:, j, :],
+                    scalar1=damping[chunk[1]][:, j : j + 1], scalar2=None, op0=MULT,
                 )
-            raw[key] = damped
 
-        def interleave(key, half):
-            piece = key + str(half)
-            grouped[piece] = work.tile([P, 2 * KP], BF16, name="grouped", bufs=6, align_bytes=64)
-            if key[0] == "k":
-                src = raw[key][:].rearrange("p j (m t i) -> p m t j i", t=PACK, i=RUN)[:, :, 2 * half : 2 * half + 2, :, :]
-                dst = grouped[piece][:].rearrange("p (t m i j) -> p m t j i", t=2, i=RUN, j=PACK)
+        def interleave(chunk, copy, lo, hi):
+            if chunk not in grouped:
+                name = "grouped%d" % (chunks.index(chunk) % GROUPED_BUFS)
+                grouped[chunk] = keep.tile([P, SLOTS * KP], BF16, name=name, align_bytes=64)
+            dst = grouped[chunk][:, 2 * KP * lo : 2 * KP * hi]
+            if chunk[0] == "ket":
+                src = raw[chunk][:].rearrange("p j (m t i) -> p m t j i", t=SLOTS, i=RUN)[:, :, 2 * lo : 2 * hi, :, :]
+                dst = dst.rearrange("p (t m i j) -> p m t j i", m=P // RUN, i=RUN, j=SLOTS)
             else:
-                src = raw[key][:, :, 2 * P * half : 2 * P * (half + 1)].rearrange("p j (c i) -> p c j i", i=RUN)
-                dst = grouped[piece][:].rearrange("p (c i j) -> p c j i", i=RUN, j=PACK)
-            if (half == 1 and key not in ALLV.split()) or key in ALLS.split():
-                nc.scalar.copy(out=dst, in_=src)
-            else:
-                nc.vector.tensor_copy(out=dst, in_=src)
+                src = raw[chunk][:, :, 2 * P * lo : 2 * P * hi].rearrange("p j (c i) -> p c j i", i=RUN)
+                dst = dst.rearrange("p (c i j) -> p c j i", i=RUN, j=SLOTS)
+            copy(out=dst, in_=src)
 
-        def quantize(key, values, width):
-            codes[key] = keep.tile([P, width], U32, name="codes_" + key, align_bytes=64)
-            planes[key] = keep.tile([P, width], U8, name="plane_" + key, align_bytes=64)
+        def quantize(key, name, values, width):
+            codes[key] = keep.tile([P, width], U32, name="codes_" + name, align_bytes=64)
+            planes[key] = keep.tile([P, width], U8, name="plane_" + name, align_bytes=64)
             nc.vector.quantize_mx(out=codes[key][:].bitcast(FP8X4), scales=planes[key][:], in_=values)
 
-        def permute_l(g):
-            l_codes[g] = keep.tile([P, XP, PACK, 2 * P], U8, name="l_codes%d" % g, align_bytes=64)
-            l_plane[g] = keep.tile([P, XP, PACK, P], U8, name="l_plane%d" % g, align_bytes=64)
+        def quantize_chunk(chunk):
+            quantize(chunk, "%s%d%d" % chunk, grouped[chunk][:], KP)
+
+        def quantize_z(g):
+            quantize(("z", g), "z%d" % g, z_bf[g][:].rearrange("p n t -> p (n t)"), NS)
+
+        def sort_l(g):
+            l_codes[g] = keep.tile([P, X_PASSES, SLOTS, 2 * P], U8, name="l_codes%d" % g, align_bytes=64)
+            l_plane[g] = keep.tile([P, X_PASSES, SLOTS, P], U8, name="l_plane%d" % g, align_bytes=64)
             nc.vector.tensor_copy(
                 out=l_codes[g][:].bitcast(I32).rearrange("p x t (m w) -> p x t m w", w=2),
-                in_=l_raw[g][:].bitcast(I32).rearrange("p x (m t w) -> p x t m w", t=PACK, w=2),
+                in_=l_raw[g][:].bitcast(I32).rearrange("p x (m t w) -> p x t m w", t=SLOTS, w=2),
             )
             nc.vector.tensor_copy(
                 out=l_plane[g][:].bitcast(I32),
-                in_=l_rows[:, :, KP * g : KP * (g + 1)].bitcast(I32).rearrange("p x (m t) -> p x t m", t=PACK),
+                in_=l_rows[:, :, KP * g : KP * (g + 1)].bitcast(I32).rearrange("p x (m t) -> p x t m", t=SLOTS),
             )
 
-        banks = {}
-        zq = []
-        vir_sb = {}
-        a_bf = {}
+        def mx_pass(acc, lhs, lhs_cols, rhs, rhs_cols, start, stop):
+            nc.tensor.matmul_mx(
+                out=acc,
+                lhsT=codes[lhs][:, lhs_cols].bitcast(FP8X4), lhsT_scale=planes[lhs][:, lhs_cols],
+                rhs=codes[rhs][:, rhs_cols].bitcast(FP8X4), rhs_scale=planes[rhs][:, rhs_cols],
+                start=start, stop=stop,
+            )
 
-        def bank(name):
-            return psum.tile([P, PACK, P], F32, name=name, tag="bank", bufs=8)
+        def cols(index, width):
+            return slice(width * index, width * (index + 1))
 
-        def pe(job):
-            kind = job[0]
-            if kind == "Z":
-                g, sc = int(job[1]), int(job[2])
-                banks[job] = bank("z_ps")
-                for t in range(PACK):
-                    for x in range(XP):
+        occ_jobs = [("occ", g, u) for g in range(GROUPS) for u in range(TILES // 2)]
+        occ_jobs = occ_jobs + [("occ", g, u) for u in range(TILES // 2, TILES) for g in range(GROUPS)]
+        a_sets = [occ_jobs[n : n + 2] for n in range(0, len(occ_jobs) - 2, 2)] + [[job] for job in occ_jobs[-2:]]
+        a_set_of = {job: n for n, members in enumerate(a_sets) for job in members}
+
+        def multiply(job):
+            banks[job] = psum.tile([P, KP], F32, name="bank")
+            acc = banks[job]
+            if job[0] == "z":
+                g, quarter = job[1:]
+                for t in range(SLOTS):
+                    for x in range(X_PASSES):
                         nc.tensor.matmul_mx(
-                            out=banks[job][:, t, :],
+                            out=acc[:, cols(t, P)],
                             lhsT=l_codes[g][:, x, t, :].bitcast(FP4X4), lhsT_scale=l_plane[g][:, x, t, :],
-                            rhs=r_codes[:, x, 2 * P * sc : 2 * P * (sc + 1)].bitcast(FP4X4),
-                            rhs_scale=r_plane[:, x, P * sc : P * (sc + 1)],
-                            start=(x == 0), stop=(x == XP - 1),
+                            rhs=r_codes[:, x, cols(quarter, 2 * P)].bitcast(FP4X4),
+                            rhs_scale=r_plane[:, x, cols(quarter, P)],
+                            start=(x == 0), stop=(x == X_PASSES - 1),
                         )
-            elif kind == "V":
-                g, q, tp = int(job[1]), int(job[2]), int(job[3])
-                banks[job] = psum.tile([P, 2, 2 * P], F32, name="vir_ps", tag="bank", bufs=8)
+            elif job[0] == "vir":
+                g, pair, tp = job[1:]
                 for t in range(2):
-                    for c in (1, 2):
-                        ket, bra = "k%d%d%d" % (c, g, tp), "b%d%d%d" % (c, q // 2, q % 2)
-                        nc.tensor.matmul_mx(
-                            out=banks[job][:, t, :],
-                            lhsT=codes[ket][:, P * t : P * (t + 1)].bitcast(FP8X4),
-                            lhsT_scale=planes[ket][:, P * t : P * (t + 1)],
-                            rhs=codes[bra][:].bitcast(FP8X4), rhs_scale=planes[bra][:],
-                            start=(c == 1), stop=(c == 2),
+                    for c in (VIR_A, VIR_B):
+                        mx_pass(
+                            acc[:, cols(t, 2 * P)], ("ket", c, g), cols(2 * tp + t, P),
+                            ("bra", c, pair // 2), cols(pair % 2, 2 * P), c == VIR_A, c == VIR_B,
                         )
-            elif kind == "C":
-                g, u = int(job[1]), int(job[2])
-                banks[job] = bank("occ_ps")
-                bra, cols = "b0%d%d" % (u // 4, u % 4 // 2), slice(P * (u % 2), P * (u % 2 + 1))
-                for t in range(PACK):
-                    ket, kc = "k0%d%d" % (g, t // 2), slice(P * (t % 2), P * (t % 2 + 1))
-                    nc.tensor.matmul_mx(
-                        out=banks[job][:, t, :],
-                        lhsT=codes[ket][:, kc].bitcast(FP8X4), lhsT_scale=planes[ket][:, kc],
-                        rhs=codes[bra][:, cols].bitcast(FP8X4), rhs_scale=planes[bra][:, cols],
-                        start=True, stop=True,
+            elif job[0] == "occ":
+                g, u = job[1:]
+                for t in range(SLOTS):
+                    mx_pass(
+                        acc[:, cols(t, P)], ("ket", OCC, g), cols(t, P),
+                        ("bra", OCC, u // SLOTS), cols(u % SLOTS, P), True, True,
                     )
             else:
-                u = int(job[1])
-                banks[job] = bank("out_ps")
                 for g in range(GROUPS):
-                    a, z = "a%d%d" % (g, u), "z%d" % g
-                    nc.tensor.matmul_mx(
-                        out=banks[job][:].rearrange("p t n -> p (t n)"),
-                        lhsT=codes[a][:].bitcast(FP8X4), lhsT_scale=planes[a][:],
-                        rhs=codes[z][:].bitcast(FP8X4), rhs_scale=planes[z][:],
-                        start=(g == 0), stop=(g == GROUPS - 1),
-                    )
+                    out_pass(acc[:], job[1], g, slice(0, NS))
 
-        def drain(job):
-            kind = job[0]
-            if kind == "Z":
-                g, sc = int(job[1]), int(job[2])
-                if sc == 0:
-                    z_bf[g] = work.tile([P, S, PACK], BF16, name="z_bf", bufs=3, align_bytes=64)
-                nc.scalar.copy(out=z_bf[g][:, P * sc : P * (sc + 1), :], in_=banks[job][:].rearrange("p t n -> p n t"))
-            elif kind == "V":
-                if job[3] == "0":
-                    vir_sb[job[1:3]] = work.tile([P, 2, 2 * P, 2], F32, name="vir_sb", bufs=VIR_BUFS, align_bytes=64)
-                nc.scalar.copy(out=vir_sb[job[1:3]][:, int(job[3]), :, :], in_=banks[job][:].rearrange("p t n -> p n t"))
+        def out_pass(acc, u, g, z_cols):
+            n = a_set_of[("occ", g, u)]
+            place = a_sets[n].index(("occ", g, u))
+            mx_pass(acc, ("a", n), cols(place, P), ("z", g), z_cols, g == 0, g == GROUPS - 1)
+
+        def store(u, acc, out_cols, copy):
+            result = work.tile([P, acc.shape[1]], F32, name="result", bufs=4, align_bytes=64)
+            copy(out=result[:], in_=acc)
+            nc.sync.dma_start(out=out[cols(u, P), out_cols], in_=result[:])
+
+        def empty(job):
+            if job[0] == "z":
+                g, quarter = job[1:]
+                if quarter == 0:
+                    z_bf[g] = keep.tile([P, NS, SLOTS], BF16, name="z_bf%d" % g, align_bytes=64)
+                nc.scalar.copy(
+                    out=z_bf[g][:, cols(quarter, P), :], in_=banks[job][:].rearrange("p (t n) -> p n t", t=SLOTS)
+                )
+            elif job[0] == "vir":
+                g, pair, tp = job[1:]
+                if tp == 0:
+                    vir_sb[g, pair] = work.tile([P, 2, 2 * P, 2], F32, name="vir_sb", bufs=VIR_BUFS, align_bytes=64)
+                nc.scalar.copy(out=vir_sb[g, pair][:, tp, :, :], in_=banks[job][:].rearrange("p (t n) -> p n t", t=2))
             else:
-                u = int(job[1])
-                result = work.tile([P, PACK, P], F32, name="result", align_bytes=64)
-                nc.scalar.copy(out=result[:], in_=banks[job][:])
-                nc.sync.dma_start(out=out[P * u : P * (u + 1), :], in_=result[:].rearrange("p t n -> p (t n)"))
+                store(job[1], banks[job][:], slice(0, NS), nc.scalar.copy)
 
         def product(job):
-            u = int(job[2])
-            a_bf[job] = work.tile([P, P, 2, 2], BF16, name="a_bf", bufs=4, align_bytes=64)
-            vir = vir_sb[job[1] + str(u // 2)][:, :, P * (u % 2) : P * (u % 2 + 1), :]
+            g, u = job[1:]
+            n = a_set_of[job]
+            if job == a_sets[n][0]:
+                a_bf[n] = work.tile([P, len(a_sets[n]), P, 2, 2], BF16, name="a_bf", align_bytes=64)
             nc.vector.tensor_tensor(
-                out=a_bf[job][:],
-                in0=banks[job][:].rearrange("p (a b) n -> p n a b", b=2),
-                in1=vir.rearrange("p a n b -> p n a b"),
+                out=a_bf[n][:, a_sets[n].index(job)],
+                in0=banks[job][:].rearrange("p (a b n) -> p n a b", a=2, b=2),
+                in1=vir_sb[g, u // 2][:, :, cols(u % 2, P), :].rearrange("p a n b -> p n a b"),
                 op=MULT,
             )
 
-        def quant_a(job):
-            quantize("a" + job[1:], a_bf[job][:].rearrange("p n a b -> p (n a b)"), P)
+        def quantize_a(n):
+            values = a_bf[n][:].rearrange("p s n a b -> p (s n a b)")
+            quantize(("a", n), "a%d" % n, values, P * len(a_sets[n]))
 
-        chunks = [key for key in LOADS.split() if key[0] in "kb"]
+        half_banks = {}
 
-        def prep(k):
-            if k + 1 < len(chunks) and chunks[k + 1][0] == "b":
-                pre = chunks[k + 1]
-            else:
-                pre = None
-            if k < len(chunks):
-                interleave(chunks[k], 1)
-                interleave(chunks[k], 0)
-            if k > 0:
-                quantize(chunks[k - 1] + "1", grouped[chunks[k - 1] + "1"][:], 2 * P)
-            if pre:
-                damp(pre)
-            if k < len(chunks):
-                late.append(chunks[k] + "0")
-            load_ahead(k + 1)
+        def last_tile_passes(groups):
+            for half in range(2):
+                if half not in half_banks:
+                    half_banks[half] = psum.tile([P, KP], F32, name="bank")
+                for g in groups:
+                    out_pass(half_banks[half][:, 0 : NS // 2], TILES - 1, g, cols(half, NS // 2))
 
-        late = []
+        def last_tile_store(half, copy):
+            store(TILES - 1, half_banks[half][:, 0 : NS // 2], cols(half, NS // 2), copy)
 
-        def flush():
-            while late:
-                piece = late.pop(0)
-                quantize(piece, grouped[piece][:], 2 * P)
-
-        vir_jobs = ["V%d%d%d" % (g, q, tp) for g in range(GROUPS) for q in (0, 1) for tp in (0, 1)]
-        vir_jobs += ["V%d%d%d" % (g, q, tp) for q in (2, 3) for g in range(GROUPS) for tp in (0, 1)]
-        occ_jobs = ["C%d%d" % (g, u) for g in range(GROUPS) for u in range(4)]
-        occ_jobs += ["C%d%d" % (g, u) for u in range(4, TILES) for g in range(GROUPS)]
-        z_jobs = ["Z%d%d" % (g, sc) for g in range(GROUPS) for sc in range(PACK)]
+        scalar_jobs = []
+        for g in range(GROUPS):
+            scalar_jobs.extend(("vir", g, pair, tp) for pair in (0, 1) for tp in (0, 1))
+            scalar_jobs.extend(("z", g, quarter) for quarter in range(SLOTS))
+        scalar_jobs.extend(("vir", g, pair, tp) for pair in (2, 3) for g in range(GROUPS) for tp in (0, 1))
         jobs = []
-        outs = []
-        for i in range(len(vir_jobs) + LAG + OLAG + 1):
-            if i < len(vir_jobs):
-                jobs.append(vir_jobs[i])
-            if i >= ZPOS:
-                jobs.extend(z_jobs[ZSTEP * (i - ZPOS) : ZSTEP * (i - ZPOS + 1)])
-            if 0 <= i - LAG < len(occ_jobs):
-                jobs.append(occ_jobs[i - LAG])
-                if occ_jobs[i - LAG][1] == str(GROUPS - 1):
-                    outs.append((i + OLAG, "O" + occ_jobs[i - LAG][2]))
-            if outs and outs[0][0] <= i:
-                jobs.append(outs.pop(0)[1])
+        next_out = 0
+        for step in range(OCC_START + len(occ_jobs) + OUT_LAG):
+            jobs.extend(scalar_jobs[step : step + 1])
+            if step >= OCC_START:
+                jobs.extend(occ_jobs[step - OCC_START : step - OCC_START + 1])
+            if step >= OUT_START and next_out < TILES - 1:
+                if step >= OCC_START + occ_jobs.index(("occ", GROUPS - 1, next_out)) + OUT_LAG:
+                    jobs.append(("out", next_out))
+                    next_out = next_out + 1
 
-        if chunks[0][0] == "b":
-            damp(chunks[0])
-        for k in range(HEAD):
-            prep(k)
-            flush()
-            if 0 <= k - PERM_AT < GROUPS:
-                permute_l(k - PERM_AT)
-        k = HEAD
-        pending = []
+        def operands(job):
+            if job[0] == "z":
+                return [("sort", job[1])]
+            if job[0] == "vir":
+                return [("quant", (side, c, part)) for c in (VIR_A, VIR_B) for side, part in (("ket", job[1]), ("bra", job[2] // 2))]
+            if job[0] == "occ":
+                return [("quant", ("ket", OCC, job[1])), ("quant", ("bra", OCC, job[2] // SLOTS))]
+            return [("quant_a", a_set_of["occ", g, job[1]]) for g in range(GROUPS)] + [("quant_z", g) for g in range(GROUPS)]
+
+        tensor_queue = []
         for n, job in enumerate(jobs):
-            if n % PERIOD == 0 and k <= len(chunks):
-                prep(k)
-                if 0 <= k - PERM_AT < GROUPS:
-                    permute_l(k - PERM_AT)
-                k = k + 1
-            if job[0] == "O":
-                while any(j[2] == job[1] for j in pending):
-                    quant_a(pending.pop(0))
-            pe(job)
-            if job[0] == "C":
-                product(job)
-                if pending:
-                    quant_a(pending.pop(0))
-                pending.append(job)
-            else:
-                drain(job)
-            flush()
-            if job[0] == "Z" and job[2] == "3":
-                zq.append(job[1])
-            elif zq and n >= ZQ_AT:
-                g = zq.pop(0)
-                quantize("z" + g, z_bf[int(g)][:].rearrange("p n t -> p (n t)"), S)
+            freed = [("read", old) for old in jobs[max(n - BANKS, 0) : max(n - BANKS + 1, 0)]]
+            tensor_queue.append((job, operands(job) + freed, multiply, (job,)))
+        last_sets = [("quant_a", a_set_of["occ", g, TILES - 1]) for g in range(GROUPS)]
+        freed = [("read", old) for old in jobs[-BANKS : -BANKS + 2]]
+        tensor_queue.append(("last_first", last_sets[:-1] + freed, last_tile_passes, (range(GROUPS - 1),)))
+        tensor_queue.append(("last_done", last_sets[-1:], last_tile_passes, ([GROUPS - 1],)))
+
+        def interleave_step(chunk, copy, lo, hi):
+            k = chunks.index(chunk)
+            needs = [("quant", old) for old in chunks[max(k - GROUPED_BUFS, 0) : max(k - GROUPED_BUFS + 1, 0)]]
+            if chunk[0] == "bra":
+                needs.append(("damp", chunk))
+            return (("interleave", chunk, hi), needs, interleave, (chunk, copy, lo, hi))
+
+        vir_tiles = [job[1:3] for job in scalar_jobs if job[0] == "vir" and job[3] == 0]
+        late_halves = [interleave_step(chunk, nc.scalar.copy, lo, lo + 1) for chunk in scalar_late for lo in (0, 1)]
+        scalar_queue = [interleave_step(chunk, nc.scalar.copy, 0, 2) for chunk in scalar_early[:-1]]
+        for n, job in enumerate(job for job in jobs if job[0] != "occ"):
+            if n == FIRST_BANKS:
+                scalar_queue.append(interleave_step(scalar_early[-1], nc.scalar.copy, 0, 2))
+            if n >= LATE_START and (n - LATE_START) % LATE_EVERY == 0 and late_halves:
+                scalar_queue.append(late_halves.pop(0))
+            needs = [job]
+            if job[0] == "vir" and vir_tiles.index(job[1:3]) >= VIR_BUFS:
+                g, pair = vir_tiles[vir_tiles.index(job[1:3]) - VIR_BUFS]
+                needs.extend(("read", ("occ", g, u)) for u in (2 * pair, 2 * pair + 1))
+            scalar_queue.append((("read", job), needs, empty, (job,)))
+        scalar_queue.append(("store0", ["last_done"], last_tile_store, (0, nc.scalar.copy)))
+
+        def quantize_step(chunk):
+            return (("quant", chunk), [("interleave", chunk, 2)], quantize_chunk, (chunk,))
+
+        def z_step(g):
+            return (("quant_z", g), [("read", ("z", g, SLOTS - 1))], quantize_z, (g,))
+
+        early = chunks[: -len(scalar_late)]
+        vector_queue = [(("damp", chunks[0]), [], damp, (chunks[0],))]
+        for k in range(len(early) + QUANT_LAG):
+            ahead = k + 1 < len(chunks) and chunks[k + 1][0] == "bra"
+            if ahead and k < DAMP_FIRST:
+                vector_queue.append((("damp", chunks[k + 1]), [], damp, (chunks[k + 1],)))
+            if k < len(early) and early[k] not in scalar_early:
+                vector_queue.append(interleave_step(early[k], nc.vector.tensor_copy, 0, 2))
+            if ahead and k >= DAMP_FIRST:
+                vector_queue.append((("damp", chunks[k + 1]), [], damp, (chunks[k + 1],)))
+            if k >= QUANT_LAG:
+                vector_queue.append(quantize_step(early[k - QUANT_LAG]))
+            if k - PERM_AT in (0, 2, 4):
+                vector_queue.append((("sort", (k - PERM_AT) // 2), [], sort_l, ((k - PERM_AT) // 2,)))
+        fillers = [z_step(0), quantize_step(scalar_late[0]), z_step(1), z_step(2), quantize_step(scalar_late[1])]
+        for n, members in enumerate(a_sets):
+            for job in members:
+                needs = [job, ("read", ("vir", job[1], job[2] // 2, 1))]
+                vector_queue.append((("read", job), needs, product, (job,)))
+                if job == members[0] and n > 0:
+                    vector_queue.append((("quant_a", n - 1), [], quantize_a, (n - 1,)))
+            if fillers:
+                vector_queue.append(fillers.pop(0))
+        vector_queue.append((("quant_a", len(a_sets) - 1), [], quantize_a, (len(a_sets) - 1,)))
+        vector_queue.append(("store1", ["last_done"], last_tile_store, (1, nc.vector.tensor_copy)))
+
+        done = set()
+        queues = [tensor_queue, scalar_queue, vector_queue]
+        while any(queues):
+            ready = [queue for queue in queues if queue and all(need in done for need in queue[0][1])]
+            name, needs, step, args = ready[0].pop(0)
+            step(*args)
+            done.add(name)

@@ -20,22 +20,30 @@ KP = P * SLOTS
 GROUPS = NK // KP
 X_PASSES = NX // KP
 TILES = NB // P
-RUN = 4
+RUN = 8
 BANKS = 8
 OCC, VIR_A, VIR_B = 0, 1, 2
 
+SHARED = 0
 SCALAR_HEAD = 5
+ORDER = 0
+WIDE = 12
+ZSHIFT = 0
+SC_BACK = 3
+SC_AT = 4
+L_EVERY = 2
+SORT_LAG = 0
 FIRST_BANKS = 4
 LATE_START = 14
 LATE_EVERY = 5
 OCC_START = 21
-OUT_LAG = 5
+OUT_LAG = 4
 QUANT_LAG = 1
 DAMP_FIRST = 5
-OUT_START = 38
+OUT_START = 39
 PERM_AT = 6
 GROUPED_BUFS = 5
-VIR_BUFS = 9
+VIR_BUFS = 8
 
 
 def tile_thc_laplace_mp2_s12_kernel(
@@ -52,7 +60,22 @@ def tile_thc_laplace_mp2_s12_kernel(
         ("ket", VIR_A, 1), ("ket", VIR_B, 1), ("ket", VIR_A, 2), ("ket", VIR_B, 2),
         ("bra", VIR_A, 1), ("bra", VIR_B, 1), ("ket", OCC, 1), ("ket", OCC, 2), ("bra", OCC, 1),
     ]
-    scalar_early = chunks[0 : 2 * SCALAR_HEAD : 2]
+    if ORDER == 1:
+        chunks = [chunks[n] for n in (2, 0, 3, 1, 4, 5, 6, 7, 8, 9, 10, 11, 12, 13, 14)]
+    if ORDER == 2:
+        chunks = [chunks[n] for n in (0, 2, 1, 3, 4, 5, 6, 7, 8, 9, 10, 11, 12, 13, 14)]
+    if ORDER == 3:
+        chunks = [chunks[n] for n in (0, 1, 2, 3, 6, 7, 4, 5, 8, 9, 10, 11, 12, 13, 14)]
+    if ORDER == 4:
+        chunks = [chunks[n] for n in (0, 2, 1, 3, 6, 7, 8, 9, 4, 5, 10, 11, 12, 13, 14)]
+    if ORDER == 5:
+        chunks = [chunks[n] for n in (2, 0, 3, 1, 5, 4, 6, 7, 8, 9, 10, 11, 12, 13, 14)]
+    if ORDER == 6:
+        chunks = [chunks[n] for n in (2, 0, 3, 1, 6, 7, 8, 9, 5, 4, 10, 11, 12, 13, 14)]
+    if ORDER == 7:
+        chunks = [chunks[n] for n in (2, 0, 3, 1, 6, 7, 5, 4, 8, 9, 10, 11, 12, 13, 14)]
+    shared = chunks[:SHARED]
+    scalar_early = chunks[SHARED : SHARED + 2 * SCALAR_HEAD : 2]
     scalar_late = chunks[-2:]
 
     with ExitStack() as ctx:
@@ -94,17 +117,19 @@ def tile_thc_laplace_mp2_s12_kernel(
         for k, chunk in enumerate(chunks):
             load_chunk(chunk)
             if k == 0:
+                nc.scalar.dma_start(out=d_v[:], in_=d_vir.rearrange("(x p j) -> p x j", p=P, j=SLOTS))
+            if k == 2:
                 nc.sync.dma_start(out=d_o[:], in_=d_occ.rearrange("(p j) -> p j", j=SLOTS))
-                nc.sync.dma_start(out=d_v[:], in_=d_vir.rearrange("(x p j) -> p x j", p=P, j=SLOTS))
-            if 0 <= k - (PERM_AT - 3) < 4:
-                load_scale_rows(k - (PERM_AT - 3))
+            if 0 <= k - PERM_AT + SC_BACK < 4:
+                load_scale_rows(k - PERM_AT + SC_BACK)
             if k == PERM_AT:
                 nc.sync.dma_start(out=r_codes[:].bitcast(I32), in_=r_words.rearrange("x p n -> p x n").bitcast(I32))
-            if k - PERM_AT in (0, 2, 4):
-                load_l((k - PERM_AT) // 2)
+            if k - PERM_AT in (0, L_EVERY, 2 * L_EVERY):
+                load_l((k - PERM_AT) // L_EVERY)
 
         grouped, codes, planes = {}, {}, {}
-        l_codes, l_plane, z_bf, vir_sb, a_bf, banks = {}, {}, {}, {}, {}, {}
+        l_codes, z_bf, vir_sb, a_bf, banks = {}, {}, {}, {}, {}
+        l_plane = keep.tile([P, X_PASSES, GROUPS, SLOTS, P], U8, name="l_plane", align_bytes=64)
 
         def damp(chunk):
             for j in range(SLOTS):
@@ -139,15 +164,15 @@ def tile_thc_laplace_mp2_s12_kernel(
 
         def sort_l(g):
             l_codes[g] = keep.tile([P, X_PASSES, SLOTS, 2 * P], U8, name="l_codes%d" % g, align_bytes=64)
-            l_plane[g] = keep.tile([P, X_PASSES, SLOTS, P], U8, name="l_plane%d" % g, align_bytes=64)
             nc.vector.tensor_copy(
-                out=l_codes[g][:].bitcast(I32).rearrange("p x t (m w) -> p x t m w", w=2),
-                in_=l_raw[g][:].bitcast(I32).rearrange("p x (m t w) -> p x t m w", t=SLOTS, w=2),
+                out=l_codes[g][:].bitcast(I32).rearrange("p x t (m w) -> p x t m w", w=RUN // 2),
+                in_=l_raw[g][:].bitcast(I32).rearrange("p x (m t w) -> p x t m w", t=SLOTS, w=RUN // 2),
             )
-            nc.vector.tensor_copy(
-                out=l_plane[g][:].bitcast(I32),
-                in_=l_rows[:, :, KP * g : KP * (g + 1)].bitcast(I32).rearrange("p x (m t) -> p x t m", t=SLOTS),
-            )
+            if g == 0:
+                nc.vector.tensor_copy(
+                    out=l_plane[:].bitcast(I32).rearrange("p x g t (m w) -> p (x g) t m w", w=RUN // 4),
+                    in_=l_rows[:].bitcast(I32).rearrange("p x (g m t w) -> p (x g) t m w", g=GROUPS, t=SLOTS, w=RUN // 4),
+                )
 
         def mx_pass(acc, lhs, lhs_cols, rhs, rhs_cols, start, stop):
             nc.tensor.matmul_mx(
@@ -162,7 +187,7 @@ def tile_thc_laplace_mp2_s12_kernel(
 
         occ_jobs = [("occ", g, u) for g in range(GROUPS) for u in range(TILES // 2)]
         occ_jobs = occ_jobs + [("occ", g, u) for u in range(TILES // 2, TILES) for g in range(GROUPS)]
-        a_sets = [occ_jobs[n : n + 2] for n in range(0, len(occ_jobs) - 2, 2)] + [[job] for job in occ_jobs[-2:]]
+        a_sets = [occ_jobs[n : n + 4] for n in range(0, WIDE, 4)] + [occ_jobs[n : n + 2] for n in range(WIDE, len(occ_jobs) - 2, 2)] + [[job] for job in occ_jobs[-2:]]
         a_set_of = {job: n for n, members in enumerate(a_sets) for job in members}
 
         def multiply(job):
@@ -174,7 +199,7 @@ def tile_thc_laplace_mp2_s12_kernel(
                     for x in range(X_PASSES):
                         nc.tensor.matmul_mx(
                             out=acc[:, cols(t, P)],
-                            lhsT=l_codes[g][:, x, t, :].bitcast(FP4X4), lhsT_scale=l_plane[g][:, x, t, :],
+                            lhsT=l_codes[g][:, x, t, :].bitcast(FP4X4), lhsT_scale=l_plane[:, x, g, t, :],
                             rhs=r_codes[:, x, cols(quarter, 2 * P)].bitcast(FP4X4),
                             rhs_scale=r_plane[:, x, cols(quarter, P)],
                             start=(x == 0), stop=(x == X_PASSES - 1),
@@ -253,9 +278,11 @@ def tile_thc_laplace_mp2_s12_kernel(
             store(TILES - 1, half_banks[half][:, 0 : NS // 2], cols(half, NS // 2), copy)
 
         scalar_jobs = []
-        for g in range(GROUPS):
-            scalar_jobs.extend(("vir", g, pair, tp) for pair in (0, 1) for tp in (0, 1))
-            scalar_jobs.extend(("z", g, quarter) for quarter in range(SLOTS))
+        for g in range(GROUPS + ZSHIFT):
+            if g < GROUPS:
+                scalar_jobs.extend(("vir", g, pair, tp) for pair in (0, 1) for tp in (0, 1))
+            if g >= ZSHIFT:
+                scalar_jobs.extend(("z", g - ZSHIFT, quarter) for quarter in range(SLOTS))
         scalar_jobs.extend(("vir", g, pair, tp) for pair in (2, 3) for g in range(GROUPS) for tp in (0, 1))
         jobs = []
         next_out = 0
@@ -295,7 +322,8 @@ def tile_thc_laplace_mp2_s12_kernel(
 
         vir_tiles = [job[1:3] for job in scalar_jobs if job[0] == "vir" and job[3] == 0]
         late_halves = [interleave_step(chunk, nc.scalar.copy, lo, lo + 1) for chunk in scalar_late for lo in (0, 1)]
-        scalar_queue = [interleave_step(chunk, nc.scalar.copy, 0, 2) for chunk in scalar_early[:-1]]
+        scalar_queue = [interleave_step(chunk, nc.scalar.copy, 1, 2) for chunk in shared]
+        scalar_queue.extend(interleave_step(chunk, nc.scalar.copy, 0, 2) for chunk in scalar_early[:-1])
         for n, job in enumerate(job for job in jobs if job[0] != "occ"):
             if n == FIRST_BANKS:
                 scalar_queue.append(interleave_step(scalar_early[-1], nc.scalar.copy, 0, 2))
@@ -315,19 +343,20 @@ def tile_thc_laplace_mp2_s12_kernel(
             return (("quant_z", g), [("read", ("z", g, SLOTS - 1))], quantize_z, (g,))
 
         early = chunks[: -len(scalar_late)]
-        vector_queue = [(("damp", chunks[0]), [], damp, (chunks[0],))]
+        vector_queue = [(("damp", chunk), [], damp, (chunk,)) for chunk in chunks[:1] if chunk[0] == "bra"]
         for k in range(len(early) + QUANT_LAG):
             ahead = k + 1 < len(chunks) and chunks[k + 1][0] == "bra"
             if ahead and k < DAMP_FIRST:
                 vector_queue.append((("damp", chunks[k + 1]), [], damp, (chunks[k + 1],)))
             if k < len(early) and early[k] not in scalar_early:
-                vector_queue.append(interleave_step(early[k], nc.vector.tensor_copy, 0, 2))
+                vector_queue.append(interleave_step(early[k], nc.vector.tensor_copy, 0, 1 if early[k] in shared else 2))
             if ahead and k >= DAMP_FIRST:
                 vector_queue.append((("damp", chunks[k + 1]), [], damp, (chunks[k + 1],)))
             if k >= QUANT_LAG:
                 vector_queue.append(quantize_step(early[k - QUANT_LAG]))
-            if k - PERM_AT in (0, 2, 4):
-                vector_queue.append((("sort", (k - PERM_AT) // 2), [], sort_l, ((k - PERM_AT) // 2,)))
+            if k - PERM_AT - SORT_LAG in (0, L_EVERY, 2 * L_EVERY):
+                g = (k - PERM_AT - SORT_LAG) // L_EVERY
+                vector_queue.append((("sort", g), [], sort_l, (g,)))
         fillers = [z_step(0), quantize_step(scalar_late[0]), z_step(1), z_step(2), quantize_step(scalar_late[1])]
         for n, members in enumerate(a_sets):
             for job in members:
@@ -335,8 +364,8 @@ def tile_thc_laplace_mp2_s12_kernel(
                 vector_queue.append((("read", job), needs, product, (job,)))
                 if job == members[0] and n > 0:
                     vector_queue.append((("quant_a", n - 1), [], quantize_a, (n - 1,)))
-            if fillers:
-                vector_queue.append(fillers.pop(0))
+                if fillers and occ_jobs.index(job) % 2 == 1:
+                    vector_queue.append(fillers.pop(0))
         vector_queue.append((("quant_a", len(a_sets) - 1), [], quantize_a, (len(a_sets) - 1,)))
         vector_queue.append(("store1", ["last_done"], last_tile_store, (1, nc.vector.tensor_copy)))
 

from contextlib import ExitStack

import concourse.mybir as mybir

NO, NV, NX, NB, NK, NS = 512, 1024, 1024, 1024, 1536, 512
FLOPS = 2 * (NO + NV) * NB * NK + 2 * NX * NK * NS + 2 * NB * NK * NS

F32 = mybir.dt.float32
BF16 = mybir.dt.bfloat16
I32 = mybir.dt.int32
U32 = mybir.dt.uint32
U8 = mybir.dt.uint8
FP8X4 = mybir.dt.float8_e4m3fn_x4
FP4X4 = mybir.dt.float4_e2m1fn_x4
MULT = mybir.AluOpType.mult

P = 128
SLOTS = 4
KP = P * SLOTS
GROUPS = NK // KP
X_PASSES = NX // KP
TILES = NB // P
RUN = 8
BANKS = 8
OCC, VIR_A, VIR_B = 0, 1, 2

SHARED = 0
SCALAR_HEAD = 5
ORDER = 0
WIDE = 12
ZSHIFT = 0
SC_BACK = 3
SC_AT = 4
L_EVERY = 2
SORT_LAG = 0
FIRST_BANKS = 4
LATE_START = 14
LATE_EVERY = 5
OCC_START = 21
OUT_LAG = 4
QUANT_LAG = 1
DAMP_FIRST = 5
OUT_START = 39
PERM_AT = 6
GROUPED_BUFS = 5
VIR_BUFS = 8


def tile_thc_laplace_mp2_s12_kernel(
    tc, xo_bra, xo_ket, d_occ, xv_bra, xv_ket, d_vir, l_words, l_scales, r_words, r_scales, out
):
    nc = tc.nc
    rows_of = {
        "ket": [xo_ket, xv_ket[0:KP, :], xv_ket[KP:, :]],
        "bra": [xo_bra, xv_bra[0:KP, :], xv_bra[KP:, :]],
    }
    chunks = [
        ("bra", VIR_A, 0), ("bra", VIR_B, 0), ("ket", VIR_A, 0), ("ket", VIR_B, 0),
        ("bra", OCC, 0), ("ket", OCC, 0),
        ("ket", VIR_A, 1), ("ket", VIR_B, 1), ("ket", VIR_A, 2), ("ket", VIR_B, 2),
        ("bra", VIR_A, 1), ("bra", VIR_B, 1), ("ket", OCC, 1), ("ket", OCC, 2), ("bra", OCC, 1),
    ]
    if ORDER == 1:
        chunks = [chunks[n] for n in (2, 0, 3, 1, 4, 5, 6, 7, 8, 9, 10, 11, 12, 13, 14)]
    if ORDER == 2:
        chunks = [chunks[n] for n in (0, 2, 1, 3, 4, 5, 6, 7, 8, 9, 10, 11, 12, 13, 14)]
    if ORDER == 3:
        chunks = [chunks[n] for n in (0, 1, 2, 3, 6, 7, 4, 5, 8, 9, 10, 11, 12, 13, 14)]
    if ORDER == 4:
        chunks = [chunks[n] for n in (0, 2, 1, 3, 6, 7, 8, 9, 4, 5, 10, 11, 12, 13, 14)]
    if ORDER == 5:
        chunks = [chunks[n] for n in (2, 0, 3, 1, 5, 4, 6, 7, 8, 9, 10, 11, 12, 13, 14)]
    if ORDER == 6:
        chunks = [chunks[n] for n in (2, 0, 3, 1, 6, 7, 8, 9, 5, 4, 10, 11, 12, 13, 14)]
    if ORDER == 7:
        chunks = [chunks[n] for n in (2, 0, 3, 1, 6, 7, 5, 4, 8, 9, 10, 11, 12, 13, 14)]
    shared = chunks[:SHARED]
    scalar_early = chunks[SHARED : SHARED + 2 * SCALAR_HEAD : 2]
    scalar_late = chunks[-2:]

    with ExitStack() as ctx:
        keep = ctx.enter_context(tc.tile_pool(name="keep", bufs=1))
        work = ctx.enter_context(tc.tile_pool(name="work", bufs=3))
        psum = ctx.enter_context(tc.psum_pool(name="psum", bufs=BANKS))
        ctx.enter_context(tc.manual_schedule())

        l_rows = keep.tile([P, X_PASSES, NK], U8, name="l_rows", align_bytes=64)
        r_plane = keep.tile([P, X_PASSES, NS], U8, name="r_plane", align_bytes=64)
        nc.vector.memset(l_rows[:].rearrange("p x n -> p (x n)").bitcast(I32), 0)
        nc.vector.memset(r_plane[:].rearrange("p x n -> p (x n)").bitcast(I32), 0)

        r_codes = keep.tile([P, X_PASSES, 2 * NS], U8, name="r_codes", align_bytes=64)
        d_o = keep.tile([P, SLOTS], BF16, name="d_o")
        d_v = keep.tile([P, X_PASSES, SLOTS], BF16, name="d_v")
        damping = [d_o[:, :], d_v[:, 0, :], d_v[:, 1, :]]
        raw = {}
        l_raw = {}

        def load_chunk(chunk):
            side, c, part = chunk
            raw[chunk] = keep.tile([P, SLOTS, KP], BF16, name="raw_%s%d%d" % chunk, align_bytes=64)
            rows = rows_of[side][c][:, KP * part : KP * (part + 1)]
            nc.sync.dma_start(out=raw[chunk][:], in_=rows.rearrange("(p j) w -> p j w", j=SLOTS))

        def load_scale_rows(r):
            for plane, scales in ((l_rows, l_scales), (r_plane, r_scales)):
                nc.sync.dma_start(
                    out=plane[r:P:32, :, :].bitcast(I32),
                    in_=scales[:, r:16:4, :].rearrange("x q n -> q x n").bitcast(I32),
                )

        def load_l(g):
            l_raw[g] = keep.tile([P, X_PASSES, 2 * KP], U8, name="l_raw%d" % g, align_bytes=64)
            words = l_words[:, :, 2 * KP * g : 2 * KP * (g + 1)]
            nc.sync.dma_start(out=l_raw[g][:].bitcast(I32), in_=words.rearrange("x p n -> p x n").bitcast(I32))

        for k, chunk in enumerate(chunks):
            load_chunk(chunk)
            if k == 0:
                nc.scalar.dma_start(out=d_v[:], in_=d_vir.rearrange("(x p j) -> p x j", p=P, j=SLOTS))
            if k == 2:
                nc.sync.dma_start(out=d_o[:], in_=d_occ.rearrange("(p j) -> p j", j=SLOTS))
            if 0 <= k - PERM_AT + SC_BACK < 4:
                load_scale_rows(k - PERM_AT + SC_BACK)
            if k == PERM_AT:
                nc.sync.dma_start(out=r_codes[:].bitcast(I32), in_=r_words.rearrange("x p n -> p x n").bitcast(I32))
            if k - PERM_AT in (0, L_EVERY, 2 * L_EVERY):
                load_l((k - PERM_AT) // L_EVERY)

        grouped, codes, planes = {}, {}, {}
        l_codes, z_bf, vir_sb, a_bf, banks = {}, {}, {}, {}, {}
        l_plane = keep.tile([P, X_PASSES, GROUPS, SLOTS, P], U8, name="l_plane", align_bytes=64)

        def damp(chunk):
            for j in range(SLOTS):
                nc.vector.tensor_scalar(
                    out=raw[chunk][:, j, :], in0=raw[chunk][:, j, :],
                    scalar1=damping[chunk[1]][:, j : j + 1], scalar2=None, op0=MULT,
                )

        def interleave(chunk, copy, lo, hi):
            if chunk not in grouped:
                name = "grouped%d" % (chunks.index(chunk) % GROUPED_BUFS)
                grouped[chunk] = keep.tile([P, SLOTS * KP], BF16, name=name, align_bytes=64)
            dst = grouped[chunk][:, 2 * KP * lo : 2 * KP * hi]
            if chunk[0] == "ket":
                src = raw[chunk][:].rearrange("p j (m t i) -> p m t j i", t=SLOTS, i=RUN)[:, :, 2 * lo : 2 * hi, :, :]
                dst = dst.rearrange("p (t m i j) -> p m t j i", m=P // RUN, i=RUN, j=SLOTS)
            else:
                src = raw[chunk][:, :, 2 * P * lo : 2 * P * hi].rearrange("p j (c i) -> p c j i", i=RUN)
                dst = dst.rearrange("p (c i j) -> p c j i", i=RUN, j=SLOTS)
            copy(out=dst, in_=src)

        def quantize(key, name, values, width):
            codes[key] = keep.tile([P, width], U32, name="codes_" + name, align_bytes=64)
            planes[key] = keep.tile([P, width], U8, name="plane_" + name, align_bytes=64)
            nc.vector.quantize_mx(out=codes[key][:].bitcast(FP8X4), scales=planes[key][:], in_=values)

        def quantize_chunk(chunk):
            quantize(chunk, "%s%d%d" % chunk, grouped[chunk][:], KP)

        def quantize_z(g):
            quantize(("z", g), "z%d" % g, z_bf[g][:].rearrange("p n t -> p (n t)"), NS)

        def sort_l(g):
            l_codes[g] = keep.tile([P, X_PASSES, SLOTS, 2 * P], U8, name="l_codes%d" % g, align_bytes=64)
            nc.vector.tensor_copy(
                out=l_codes[g][:].bitcast(I32).rearrange("p x t (m w) -> p x t m w", w=RUN // 2),
                in_=l_raw[g][:].bitcast(I32).rearrange("p x (m t w) -> p x t m w", t=SLOTS, w=RUN // 2),
            )
            if g == 0:
                nc.vector.tensor_copy(
                    out=l_plane[:].bitcast(I32).rearrange("p x g t (m w) -> p (x g) t m w", w=RUN // 4),
                    in_=l_rows[:].bitcast(I32).rearrange("p x (g m t w) -> p (x g) t m w", g=GROUPS, t=SLOTS, w=RUN // 4),
                )

        def mx_pass(acc, lhs, lhs_cols, rhs, rhs_cols, start, stop):
            nc.tensor.matmul_mx(
                out=acc,
                lhsT=codes[lhs][:, lhs_cols].bitcast(FP8X4), lhsT_scale=planes[lhs][:, lhs_cols],
                rhs=codes[rhs][:, rhs_cols].bitcast(FP8X4), rhs_scale=planes[rhs][:, rhs_cols],
                start=start, stop=stop,
            )

        def cols(index, width):
            return slice(width * index, width * (index + 1))

        occ_jobs = [("occ", g, u) for g in range(GROUPS) for u in range(TILES // 2)]
        occ_jobs = occ_jobs + [("occ", g, u) for u in range(TILES // 2, TILES) for g in range(GROUPS)]
        a_sets = [occ_jobs[n : n + 4] for n in range(0, WIDE, 4)] + [occ_jobs[n : n + 2] for n in range(WIDE, len(occ_jobs) - 2, 2)] + [[job] for job in occ_jobs[-2:]]
        a_set_of = {job: n for n, members in enumerate(a_sets) for job in members}

        def multiply(job):
            banks[job] = psum.tile([P, KP], F32, name="bank")
            acc = banks[job]
            if job[0] == "z":
                g, quarter = job[1:]
                for t in range(SLOTS):
                    for x in range(X_PASSES):
                        nc.tensor.matmul_mx(
                            out=acc[:, cols(t, P)],
                            lhsT=l_codes[g][:, x, t, :].bitcast(FP4X4), lhsT_scale=l_plane[:, x, g, t, :],
                            rhs=r_codes[:, x, cols(quarter, 2 * P)].bitcast(FP4X4),
                            rhs_scale=r_plane[:, x, cols(quarter, P)],
                            start=(x == 0), stop=(x == X_PASSES - 1),
                        )
            elif job[0] == "vir":
                g, pair, tp = job[1:]
                for t in range(2):
                    for c in (VIR_A, VIR_B):
                        mx_pass(
                            acc[:, cols(t, 2 * P)], ("ket", c, g), cols(2 * tp + t, P),
                            ("bra", c, pair // 2), cols(pair % 2, 2 * P), c == VIR_A, c == VIR_B,
                        )
            elif job[0] == "occ":
                g, u = job[1:]
                for t in range(SLOTS):
                    mx_pass(
                        acc[:, cols(t, P)], ("ket", OCC, g), cols(t, P),
                        ("bra", OCC, u // SLOTS), cols(u % SLOTS, P), True, True,
                    )
            else:
                for g in range(GROUPS):
                    out_pass(acc[:], job[1], g, slice(0, NS))

        def out_pass(acc, u, g, z_cols):
            n = a_set_of[("occ", g, u)]
            place = a_sets[n].index(("occ", g, u))
            mx_pass(acc, ("a", n), cols(place, P), ("z", g), z_cols, g == 0, g == GROUPS - 1)

        def store(u, acc, out_cols, copy):
            result = work.tile([P, acc.shape[1]], F32, name="result", bufs=4, align_bytes=64)
            copy(out=result[:], in_=acc)
            nc.sync.dma_start(out=out[cols(u, P), out_cols], in_=result[:])

        def empty(job):
            if job[0] == "z":
                g, quarter = job[1:]
                if quarter == 0:
                    z_bf[g] = keep.tile([P, NS, SLOTS], BF16, name="z_bf%d" % g, align_bytes=64)
                nc.scalar.copy(
                    out=z_bf[g][:, cols(quarter, P), :], in_=banks[job][:].rearrange("p (t n) -> p n t", t=SLOTS)
                )
            elif job[0] == "vir":
                g, pair, tp = job[1:]
                if tp == 0:
                    vir_sb[g, pair] = work.tile([P, 2, 2 * P, 2], F32, name="vir_sb", bufs=VIR_BUFS, align_bytes=64)
                nc.scalar.copy(out=vir_sb[g, pair][:, tp, :, :], in_=banks[job][:].rearrange("p (t n) -> p n t", t=2))
            else:
                store(job[1], banks[job][:], slice(0, NS), nc.scalar.copy)

        def product(job):
            g, u = job[1:]
            n = a_set_of[job]
            if job == a_sets[n][0]:
                a_bf[n] = work.tile([P, len(a_sets[n]), P, 2, 2], BF16, name="a_bf", align_bytes=64)
            nc.vector.tensor_tensor(
                out=a_bf[n][:, a_sets[n].index(job)],
                in0=banks[job][:].rearrange("p (a b n) -> p n a b", a=2, b=2),
                in1=vir_sb[g, u // 2][:, :, cols(u % 2, P), :].rearrange("p a n b -> p n a b"),
                op=MULT,
            )

        def quantize_a(n):
            values = a_bf[n][:].rearrange("p s n a b -> p (s n a b)")
            quantize(("a", n), "a%d" % n, values, P * len(a_sets[n]))

        half_banks = {}

        def last_tile_passes(groups):
            for half in range(2):
                if half not in half_banks:
                    half_banks[half] = psum.tile([P, KP], F32, name="bank")
                for g in groups:
                    out_pass(half_banks[half][:, 0 : NS // 2], TILES - 1, g, cols(half, NS // 2))

        def last_tile_store(half, copy):
            store(TILES - 1, half_banks[half][:, 0 : NS // 2], cols(half, NS // 2), copy)

        scalar_jobs = []
        for g in range(GROUPS + ZSHIFT):
            if g < GROUPS:
                scalar_jobs.extend(("vir", g, pair, tp) for pair in (0, 1) for tp in (0, 1))
            if g >= ZSHIFT:
                scalar_jobs.extend(("z", g - ZSHIFT, quarter) for quarter in range(SLOTS))
        scalar_jobs.extend(("vir", g, pair, tp) for pair in (2, 3) for g in range(GROUPS) for tp in (0, 1))
        jobs = []
        next_out = 0
        for step in range(OCC_START + len(occ_jobs) + OUT_LAG):
            jobs.extend(scalar_jobs[step : step + 1])
            if step >= OCC_START:
                jobs.extend(occ_jobs[step - OCC_START : step - OCC_START + 1])
            if step >= OUT_START and next_out < TILES - 1:
                if step >= OCC_START + occ_jobs.index(("occ", GROUPS - 1, next_out)) + OUT_LAG:
                    jobs.append(("out", next_out))
                    next_out = next_out + 1

        def operands(job):
            if job[0] == "z":
                return [("sort", job[1])]
            if job[0] == "vir":
                return [("quant", (side, c, part)) for c in (VIR_A, VIR_B) for side, part in (("ket", job[1]), ("bra", job[2] // 2))]
            if job[0] == "occ":
                return [("quant", ("ket", OCC, job[1])), ("quant", ("bra", OCC, job[2] // SLOTS))]
            return [("quant_a", a_set_of["occ", g, job[1]]) for g in range(GROUPS)] + [("quant_z", g) for g in range(GROUPS)]

        tensor_queue = []
        for n, job in enumerate(jobs):
            freed = [("read", old) for old in jobs[max(n - BANKS, 0) : max(n - BANKS + 1, 0)]]
            tensor_queue.append((job, operands(job) + freed, multiply, (job,)))
        last_sets = [("quant_a", a_set_of["occ", g, TILES - 1]) for g in range(GROUPS)]
        freed = [("read", old) for old in jobs[-BANKS : -BANKS + 2]]
        tensor_queue.append(("last_first", last_sets[:-1] + freed, last_tile_passes, (range(GROUPS - 1),)))
        tensor_queue.append(("last_done", last_sets[-1:], last_tile_passes, ([GROUPS - 1],)))

        def interleave_step(chunk, copy, lo, hi):
            k = chunks.index(chunk)
            needs = [("quant", old) for old in chunks[max(k - GROUPED_BUFS, 0) : max(k - GROUPED_BUFS + 1, 0)]]
            if chunk[0] == "bra":
                needs.append(("damp", chunk))
            return (("interleave", chunk, hi), needs, interleave, (chunk, copy, lo, hi))

        vir_tiles = [job[1:3] for job in scalar_jobs if job[0] == "vir" and job[3] == 0]
        late_halves = [interleave_step(chunk, nc.scalar.copy, lo, lo + 1) for chunk in scalar_late for lo in (0, 1)]
        scalar_queue = [interleave_step(chunk, nc.scalar.copy, 1, 2) for chunk in shared]
        scalar_queue.extend(interleave_step(chunk, nc.scalar.copy, 0, 2) for chunk in scalar_early[:-1])
        for n, job in enumerate(job for job in jobs if job[0] != "occ"):
            if n == FIRST_BANKS:
                scalar_queue.append(interleave_step(scalar_early[-1], nc.scalar.copy, 0, 2))
            if n >= LATE_START and (n - LATE_START) % LATE_EVERY == 0 and late_halves:
                scalar_queue.append(late_halves.pop(0))
            needs = [job]
            if job[0] == "vir" and vir_tiles.index(job[1:3]) >= VIR_BUFS:
                g, pair = vir_tiles[vir_tiles.index(job[1:3]) - VIR_BUFS]
                needs.extend(("read", ("occ", g, u)) for u in (2 * pair, 2 * pair + 1))
            scalar_queue.append((("read", job), needs, empty, (job,)))
        scalar_queue.append(("store0", ["last_done"], last_tile_store, (0, nc.scalar.copy)))

        def quantize_step(chunk):
            return (("quant", chunk), [("interleave", chunk, 2)], quantize_chunk, (chunk,))

        def z_step(g):
            return (("quant_z", g), [("read", ("z", g, SLOTS - 1))], quantize_z, (g,))

        early = chunks[: -len(scalar_late)]
        vector_queue = [(("damp", chunk), [], damp, (chunk,)) for chunk in chunks[:1] if chunk[0] == "bra"]
        for k in range(len(early) + QUANT_LAG):
            ahead = k + 1 < len(chunks) and chunks[k + 1][0] == "bra"
            if ahead and k < DAMP_FIRST:
                vector_queue.append((("damp", chunks[k + 1]), [], damp, (chunks[k + 1],)))
            if k < len(early) and early[k] not in scalar_early:
                vector_queue.append(interleave_step(early[k], nc.vector.tensor_copy, 0, 1 if early[k] in shared else 2))
            if ahead and k >= DAMP_FIRST:
                vector_queue.append((("damp", chunks[k + 1]), [], damp, (chunks[k + 1],)))
            if k >= QUANT_LAG:
                vector_queue.append(quantize_step(early[k - QUANT_LAG]))
            if k - PERM_AT - SORT_LAG in (0, L_EVERY, 2 * L_EVERY):
                g = (k - PERM_AT - SORT_LAG) // L_EVERY
                vector_queue.append((("sort", g), [], sort_l, (g,)))
        fillers = [z_step(0), quantize_step(scalar_late[0]), z_step(1), z_step(2), quantize_step(scalar_late[1])]
        for n, members in enumerate(a_sets):
            for job in members:
                needs = [job, ("read", ("vir", job[1], job[2] // 2, 1))]
                vector_queue.append((("read", job), needs, product, (job,)))
                if job == members[0] and n > 0:
                    vector_queue.append((("quant_a", n - 1), [], quantize_a, (n - 1,)))
                if fillers and occ_jobs.index(job) % 2 == 1:
                    vector_queue.append(fillers.pop(0))
        vector_queue.append((("quant_a", len(a_sets) - 1), [], quantize_a, (len(a_sets) - 1,)))
        vector_queue.append(("store1", ["last_done"], last_tile_store, (1, nc.vector.tensor_copy)))

        done = set()
        queues = [tensor_queue, scalar_queue, vector_queue]
        while any(queues):
            ready = [queue for queue in queues if queue and all(need in done for need in queue[0][1])]
            name, needs, step, args = ready[0].pop(0)
            step(*args)
            done.add(name)
